import numpy as np
import ml_dtypes


def mxq(x, axis, fmt="e4m3"):
    dtype, down = {"e4m3": (ml_dtypes.float8_e4m3fn, 7), "e5m2": (ml_dtypes.float8_e5m2, 14)}[fmt]
    v = np.moveaxis(np.asarray(x, np.float32).astype(ml_dtypes.bfloat16).astype(np.float64), axis, -1)
    blocks = v.reshape(v.shape[:-1] + (-1, 32))
    amax = np.abs(blocks).max(-1, keepdims=True)
    byte = np.maximum(np.where(amax > 0, np.frexp(amax)[1] - 1 + 127, 0) - down, 1)
    scale = np.exp2(byte - 127.0)
    codes = (blocks / scale).astype(np.float32).astype(dtype).astype(np.float64)
    return np.moveaxis((codes * scale).reshape(v.shape), -1, axis)


WIDE = False


def mx_kscale(k):
    if not WIDE:
        return np.ones(k)
    levels = np.array([10, -10, 5, -5, 0])
    if k % 512:
        return np.exp2(np.random.permutation(np.resize(levels, k // 32))).repeat(32)
    a = np.empty((k // 512, 16))
    for p in range(k // 512):
        a[p, :8] = np.random.permutation(np.resize(levels, 8))
        for g in range(8):
            far = levels[np.abs(levels - a[p, g]) >= 10]
            a[p, g + 8] = far[np.random.randint(len(far))]
    return np.exp2(a.ravel()).repeat(32)


def f64(x):
    return np.asarray(x).astype(np.float64)


def striped(idx):
    return np.tile(idx.reshape(-1, 16).T, (8, 1)).astype(np.uint16)


def unstriped(offs):
    return offs[:16].T.reshape(-1).astype(np.int64)


def striped8(idx):
    return np.concatenate([x.reshape(-1, 16).T for x in idx]).astype(np.uint16)


def runs(offs, k):
    lists = np.stack([offs[16 * r : 16 * r + 16].T.reshape(-1) for r in range(8)]).astype(np.int64)
    return lists[np.arange(k) % 512 // 64]


def pack_weight(w):
    k, n = w.shape
    w = f64(np.asarray(w, np.float32).astype(ml_dtypes.bfloat16)).reshape(k // 32, 32, n)
    amax = np.abs(w).max(1)
    byte = np.clip(np.where(amax > 0, np.frexp(amax)[1] - 1 + 127 - 7, 1), 1, 254)
    scaled = (w * np.exp2(127.0 - byte)[:, None, :]).reshape(k, n).astype(np.float32)
    words = np.ascontiguousarray(scaled.reshape(k // 512, 128, 4, n).transpose(0, 1, 3, 2)).astype(ml_dtypes.float8_e4m3fn).view(np.uint8)
    return words, np.ascontiguousarray(byte.astype(np.uint8).reshape(k // 512, 16, n))


def unpack_weight(words, scales):
    g, p, n, _ = words.shape
    vals = np.ascontiguousarray(words).view(ml_dtypes.float8_e4m3fn).astype(np.float64) * np.repeat(np.exp2(scales.astype(np.float64) - 127.0), 8, axis=1)[..., None]
    return vals.transpose(0, 1, 3, 2).reshape(g * 512, n)


K, T, S, H, C = 512, 2048, 512, 512, 512


def setup_inputs():
    n = np.random.standard_normal
    s = mx_kscale(K)[:, None]
    packed_xT = pack_weight(n((K, T)) * s)
    return {
        "x_words": packed_xT[0],
        "x_scales": packed_xT[1],
        "w1": (n((K, H)) / np.sqrt(K) / s).astype(np.float32),
        "gs": (np.random.uniform(0.5, 1.5, (K, 1)) / s).astype(np.float32),
        "offs": striped(np.random.permutation(T)[:S]),
        "n1": striped8(np.stack([np.random.permutation(S) for _ in range(8)])),
        "n2": striped8(np.stack([np.random.permutation(S) for _ in range(8)])),
        "n3": striped8(np.stack([np.random.permutation(S) for _ in range(8)])),
        "cand": striped(np.random.permutation(T)[:C]),
        "n4": striped8(np.stack([np.random.permutation(S) for _ in range(8)])),
        "n5": striped8(np.stack([np.random.permutation(S) for _ in range(8)])),
    }


def reference(x_words, x_scales, w1, gs, offs, n1, n2, n3, cand, n4, n5):
    x_cand = unpack_weight(x_words, x_scales)[:, unstriped(cand)]
    xq = unpack_weight(x_words, x_scales)[:, unstriped(offs)]
    y = mxq(f64(w1), 0, "e4m3").T @ xq
    ex = np.exp(0.5 * y)
    z = f64(gs) * (np.log((ex + ex[np.arange(H)[:, None], runs(n1, H)]) / (ex[np.arange(H)[:, None], runs(n2, H)] + ex[np.arange(H)[:, None], runs(n3, H)])))
    s = 0.0625 * ((x_cand.T @ mxq(z, 0, "e4m3")))
    st = s - (s[np.arange(C)[:, None], runs(n4, C)])
    return np.maximum(st, st[np.arange(C)[:, None], runs(n5, C)])

@@ -1,0 +1,244 @@
+from contextlib import ExitStack
+
+import concourse.mybir as mybir
+
+K, T, S, H, C = 512, 2048, 512, 512, 512
+FLOPS = 2 * K * H * S + 2 * H * C * S
+
+F32 = mybir.dt.float32
+BF16 = mybir.dt.bfloat16
+I32 = mybir.dt.int32
+U32 = mybir.dt.uint32
+U16 = mybir.dt.uint16
+U8 = mybir.dt.uint8
+FP8X4 = mybir.dt.float8_e4m3fn_x4
+ACT = mybir.ActivationFunctionType
+ALU = mybir.AluOpType
+
+P = 128
+PACK = 4
+HALF = S // 2
+WINDOW = 2 * S
+SCALAR_TILES = (2, 3)
+
+
+def tile_picked_candoddshopmx_none_p_kernel(
+    tc, x_words, x_scales, w1, gs, offs, n1, n2, n3, cand, n4, n5, out
+):
+    nc = tc.nc
+    with ExitStack() as ctx:
+        lists = ctx.enter_context(tc.tile_pool(name="lists", bufs=1))
+        keep = ctx.enter_context(tc.tile_pool(name="keep", bufs=1))
+        psum = ctx.enter_context(tc.psum_pool(name="psum", bufs=1))
+
+        def load_list(src, name):
+            tile = lists.tile([P, S // 16], U16, name=name)
+            nc.sync.dma_start(tile[:], src)
+            return tile
+
+        table_scales = keep.tile([P, T], U8, align_bytes=64)
+        nc.gpsimd.memset(table_scales[:].bitcast(I32), 0)
+        w_rows = w1.rearrange("(p j) c -> p j c", j=PACK)
+        w_raw = [keep.tile([P, PACK, H // 2], F32, name=f"w_raw{u}") for u in range(2)]
+        nc.sync.dma_start(w_raw[0][:], w_rows[:, :, : H // 2])
+        for q in range(4):
+            nc.sync.dma_start(
+                table_scales[32 * q : 32 * q + 4, :].bitcast(I32),
+                x_scales[0, 4 * q : 4 * q + 4, :].bitcast(I32),
+            )
+        offs_sb = load_list(offs, "offs_sb")
+        cand_sb = load_list(cand, "cand_sb")
+        nc.sync.dma_start(w_raw[1][:], w_rows[:, :, H // 2 :])
+        table_words = keep.tile([P, T], U32, align_bytes=64)
+        nc.sync.dma_start(
+            table_words[:].bitcast(I32), x_words[0].rearrange("p n r -> p (n r)").bitcast(I32)
+        )
+        n2_sb = load_list(n2, "n2_sb")
+        n3_sb = load_list(n3, "n3_sb")
+        n1_sb = load_list(n1, "n1_sb")
+        gain = keep.tile([P, PACK], F32)
+        nc.sync.dma_start(gain[:], gs.rearrange("(p t) o -> p (t o)", t=PACK))
+        n4_sb = load_list(n4, "n4_sb")
+        n5_sb = load_list(n5, "n5_sb")
+
+        win_a = [keep.tile([P, WINDOW], F32, name=f"win_a{t}") for t in range(PACK)]
+        win_b = [keep.tile([P, WINDOW], F32, name=f"win_b{t}") for t in range(2)]
+        for win in win_a[:3]:
+            nc.vector.memset(win[:, S:], 0.0)
+        for win in win_a[3:] + win_b:
+            nc.gpsimd.memset(win[:, S:], 0.0)
+
+        xq_scales = keep.tile([P, S], U8, align_bytes=64)
+        nc.vector.tensor_copy(xq_scales[:], table_scales[:].indirect(offs_sb[:]))
+        cand_scales_raw = keep.tile([P, C], U8, align_bytes=64)
+        nc.vector.tensor_copy(cand_scales_raw[:], table_scales[:].indirect(cand_sb[:]))
+        cand_scales = keep.tile([P, C], U8, align_bytes=64)
+        nc.vector.tensor_copy(
+            cand_scales[:].rearrange("p (t m) -> p t m", t=PACK),
+            cand_scales_raw[:].rearrange("p (m t) -> p t m", t=PACK),
+        )
+
+        w_bf = keep.tile([P, PACK, P, PACK], BF16, align_bytes=64)
+        w_walk = w_bf[:].rearrange("p t m j -> p m t j")
+        for u in range(2):
+            nc.scalar.copy(
+                w_walk[:, u * (P // 2) : (u + 1) * (P // 2)], w_raw[u][:].rearrange("p j (m t) -> p m t j", t=PACK)
+            )
+        w_words = keep.tile([P, H], U32, align_bytes=64)
+        w_scales = keep.tile([P, H], U8, align_bytes=64)
+        y_ps = [psum.tile([P, S], F32, name=f"y_ps{t}") for t in range(PACK)]
+        nc.vector.quantize_mx(
+            out=w_words[:].bitcast(FP8X4), scales=w_scales[:], in_=w_bf[:].rearrange("p t m j -> p (t m j)")
+        )
+        xq_words = keep.tile([P, S], U32, align_bytes=64)
+        nc.vector.tensor_copy(xq_words[:], table_words[:].indirect(offs_sb[:]))
+        for t in range(PACK):
+            cols = slice(t * P, (t + 1) * P)
+            nc.tensor.matmul_mx(
+                out=y_ps[t][:],
+                lhsT=w_words[:, cols].bitcast(FP8X4),
+                lhsT_scale=w_scales[:, cols],
+                rhs=xq_words[:].bitcast(FP8X4),
+                rhs_scale=xq_scales[:],
+                start=True,
+                stop=True,
+            )
+
+        cand_words_raw = keep.tile([P, C], U32, align_bytes=64)
+        nc.vector.tensor_copy(cand_words_raw[:], table_words[:].indirect(cand_sb[:]))
+        cand_words = keep.tile([P, C], U32, align_bytes=64)
+        nc.vector.tensor_copy(
+            cand_words[:].rearrange("p (t m) -> p t m", t=PACK),
+            cand_words_raw[:].rearrange("p (m t) -> p t m", t=PACK),
+        )
+
+        twin = [keep.tile([P, S], F32, name=f"twin{t}") for t in range(PACK)]
+        ex2 = [keep.tile([P, S], F32, name=f"ex2_{t}") for t in range(PACK)]
+        sums = keep.tile([P, PACK, 2, S], F32)
+        for t in range(PACK):
+            if t in SCALAR_TILES:
+                nc.scalar.activation(win_b[t % 2][:, :S], y_ps[t][:], ACT.Copy, scale=0.5)
+            nc.scalar.activation(win_a[t][:, :S], y_ps[t][:], ACT.Exp, scale=0.5)
+            nc.sync.dma_start(twin[t][:], win_a[t][:, :S])
+            if t in SCALAR_TILES:
+                nc.scalar.activation(ex2[t][:], win_b[t % 2][:].indirect(n2_sb[:]), ACT.Exp)
+
+        def denominator(t):
+            nc.vector.tensor_tensor(sums[:, t, 1, :], win_a[t][:].indirect(n3_sb[:]), ex2[t][:], ALU.add)
+
+        def numerator(t):
+            nc.vector.tensor_tensor(sums[:, t, 0, :], win_a[t][:].indirect(n1_sb[:]), twin[t][:], ALU.add)
+
+        vector_tiles = [t for t in range(PACK) if t not in SCALAR_TILES]
+        for t in vector_tiles:
+            nc.vector.tensor_copy(ex2[t][:], win_a[t][:].indirect(n2_sb[:]))
+        for t in vector_tiles:
+            denominator(t)
+        for t in vector_tiles:
+            numerator(t)
+        for t in SCALAR_TILES:
+            denominator(t)
+            numerator(t)
+
+        logs = keep.tile([P, PACK, 2, S], F32)
+        scaled = keep.tile([P, PACK, S], F32)
+        z32 = keep.tile([P, PACK, S], F32)
+        z_bf = keep.tile([P, S, PACK], BF16, align_bytes=64)
+        z_words = keep.tile([P, S], U32, align_bytes=64)
+        z_scales = keep.tile([P, S], U8, align_bytes=64)
+        whole = slice(0, S)
+        low, high = slice(0, HALF), slice(HALF, S)
+
+        def logarithms(t, cols):
+            nc.scalar.activation(logs[:, t, :, cols], sums[:, t, :, cols], ACT.Ln)
+
+        def weigh(t, cols):
+            nc.scalar.activation(scaled[:, t, cols], logs[:, t, 1, cols], ACT.Copy, scale=gain[:, t : t + 1])
+            nc.vector.scalar_tensor_tensor(
+                z32[:, t, cols], logs[:, t, 0, cols], gain[:, t : t + 1], scaled[:, t, cols], ALU.mult, ALU.subtract
+            )
+
+        logarithms(0, whole)
+        logarithms(1, whole)
+        weigh(0, whole)
+        weigh(1, whole)
+        logarithms(2, whole)
+        logarithms(3, low)
+        weigh(2, whole)
+        logarithms(3, high)
+        weigh(3, low)
+        weigh(3, high)
+
+        def walk_out(cols):
+            return z_bf[:, cols, :].rearrange("p (c i) t -> p c t i", i=4)
+
+        def walk_in(cols):
+            return z32[:, :, cols].rearrange("p t (c i) -> p c t i", i=4)
+
+        def scores(acc, t, cols):
+            rows = slice(t * P, (t + 1) * P)
+            nc.tensor.matmul_mx(
+                out=acc,
+                lhsT=cand_words[:, rows].bitcast(FP8X4),
+                lhsT_scale=cand_scales[:, rows],
+                rhs=z_words[:, cols].bitcast(FP8X4),
+                rhs_scale=z_scales[:, cols],
+                start=True,
+                stop=True,
+            )
+
+        nc.scalar.copy(walk_out(low), walk_in(low))
+        nc.vector.tensor_copy(walk_out(high), walk_in(high))
+        s_ps = [psum.tile([P, S], F32, name=f"s_ps{t}") for t in range(PACK)]
+        first_low = y_ps[0][:, low]
+        for cols, acc in ((high, s_ps[0][:, high]), (low, first_low)):
+            nc.vector.quantize_mx(
+                out=z_words[:, cols].bitcast(FP8X4),
+                scales=z_scales[:, cols],
+                in_=z_bf[:, cols, :].rearrange("p j t -> p (j t)"),
+            )
+            scores(acc, 0, cols)
+        for t in range(1, PACK):
+            scores(s_ps[t][:], t, whole)
+
+        out_rows = out.rearrange("(p t) j -> p t j", t=PACK)
+
+        def entries(cols):
+            return slice(cols.start // 16, cols.stop // 16)
+
+        def centre(t, cols):
+            nc.vector.tensor_tensor(
+                win_a[t][:, cols], win_b[t % 2][:].indirect(n4_sb[:, entries(cols)]), twin[t][:, cols], ALU.add
+            )
+
+        def centre_whole(t):
+            nc.scalar.activation(win_b[t % 2][:, :S], s_ps[t][:], ACT.Copy, scale=-0.0625)
+            nc.scalar.activation(twin[t][:], s_ps[t][:], ACT.Copy, scale=0.0625)
+            centre(t, whole)
+
+        def fetch(t, cols):
+            nc.vector.tensor_copy(ex2[t][:, cols], win_a[t][:].indirect(n5_sb[:, entries(cols)]))
+
+        def finish(t, cols):
+            nc.vector.tensor_tensor(scaled[:, t, cols], win_a[t][:, cols], ex2[t][:, cols], ALU.max)
+            nc.sync.dma_start(out_rows[:, t, cols], scaled[:, t, cols])
+
+        nc.scalar.activation(win_b[0][:, high], s_ps[0][:, high], ACT.Copy, scale=-0.0625)
+        nc.scalar.activation(twin[0][:, high], s_ps[0][:, high], ACT.Copy, scale=0.0625)
+        nc.vector.tensor_scalar(win_b[0][:, low], first_low, -0.0625, None, ALU.mult)
+        nc.scalar.activation(twin[0][:, low], first_low, ACT.Copy, scale=0.0625)
+        centre(0, high)
+        centre(0, low)
+        centre_whole(1)
+        fetch(0, whole)
+        centre_whole(2)
+        finish(0, whole)
+        fetch(1, whole)
+        centre_whole(3)
+        finish(1, whole)
+        fetch(2, whole)
+        fetch(3, low)
+        finish(2, whole)
+        fetch(3, high)
+        finish(3, low)
+        finish(3, high)

@@ -1,6 +1,7 @@
 from contextlib import ExitStack
 
 import concourse.mybir as mybir
+from concourse.masks import make_identity
 
 K, T, S, H, C = 512, 2048, 512, 512, 512
 FLOPS = 2 * K * H * S + 2 * H * C * S
@@ -68,14 +69,23 @@ def tile_picked_candoddshopmx_none_p_kernel(
         for win in win_a[3:] + win_b:
             nc.gpsimd.memset(win[:, S:], 0.0)
 
+        identity = keep.tile([P, P], F32)
+        make_identity(nc, identity[:])
+
+        whole = slice(0, S)
+        low, high = slice(0, HALF), slice(HALF, S)
+
+        def entries(cols):
+            return slice(cols.start // 16, cols.stop // 16)
+
         xq_scales = keep.tile([P, S], U8, align_bytes=64)
         nc.vector.tensor_copy(xq_scales[:], table_scales[:].indirect(offs_sb[:]))
         cand_scales_raw = keep.tile([P, C], U8, align_bytes=64)
         nc.vector.tensor_copy(cand_scales_raw[:], table_scales[:].indirect(cand_sb[:]))
         cand_scales = keep.tile([P, C], U8, align_bytes=64)
         nc.vector.tensor_copy(
-            cand_scales[:].rearrange("p (t m) -> p t m", t=PACK),
-            cand_scales_raw[:].rearrange("p (m t) -> p t m", t=PACK),
+            cand_scales[:].rearrange("p (t c i) -> p c t i", t=PACK, i=16),
+            cand_scales_raw[:].rearrange("p (c i t) -> p c t i", t=PACK, i=16),
         )
 
         w_bf = keep.tile([P, PACK, P, PACK], BF16, align_bytes=64)
@@ -108,8 +118,8 @@ def tile_picked_candoddshopmx_none_p_kernel(
         nc.vector.tensor_copy(cand_words_raw[:], table_words[:].indirect(cand_sb[:]))
         cand_words = keep.tile([P, C], U32, align_bytes=64)
         nc.vector.tensor_copy(
-            cand_words[:].rearrange("p (t m) -> p t m", t=PACK),
-            cand_words_raw[:].rearrange("p (m t) -> p t m", t=PACK),
+            cand_words[:].rearrange("p (t c i) -> p c t i", t=PACK, i=4),
+            cand_words_raw[:].rearrange("p (c i t) -> p c t i", t=PACK, i=4),
         )
 
         twin = [keep.tile([P, S], F32, name=f"twin{t}") for t in range(PACK)]
@@ -123,22 +133,26 @@ def tile_picked_candoddshopmx_none_p_kernel(
             if t in SCALAR_TILES:
                 nc.scalar.activation(ex2[t][:], win_b[t % 2][:].indirect(n2_sb[:]), ACT.Exp)
 
-        def denominator(t):
-            nc.vector.tensor_tensor(sums[:, t, 1, :], win_a[t][:].indirect(n3_sb[:]), ex2[t][:], ALU.add)
+        def denominator(t, cols):
+            nc.vector.tensor_tensor(
+                sums[:, t, 1, cols], win_a[t][:].indirect(n3_sb[:, entries(cols)]), ex2[t][:, cols], ALU.add
+            )
 
-        def numerator(t):
-            nc.vector.tensor_tensor(sums[:, t, 0, :], win_a[t][:].indirect(n1_sb[:]), twin[t][:], ALU.add)
+        def numerator(t, cols):
+            nc.vector.tensor_tensor(
+                sums[:, t, 0, cols], win_a[t][:].indirect(n1_sb[:, entries(cols)]), twin[t][:, cols], ALU.add
+            )
 
         vector_tiles = [t for t in range(PACK) if t not in SCALAR_TILES]
         for t in vector_tiles:
             nc.vector.tensor_copy(ex2[t][:], win_a[t][:].indirect(n2_sb[:]))
         for t in vector_tiles:
-            denominator(t)
+            denominator(t, whole)
         for t in vector_tiles:
-            numerator(t)
-        for t in SCALAR_TILES:
-            denominator(t)
-            numerator(t)
+            numerator(t, whole)
+        for t, cols in ((2, whole), (3, low), (3, high)):
+            denominator(t, cols)
+            numerator(t, cols)
 
         logs = keep.tile([P, PACK, 2, S], F32)
         scaled = keep.tile([P, PACK, S], F32)
@@ -146,17 +160,12 @@ def tile_picked_candoddshopmx_none_p_kernel(
         z_bf = keep.tile([P, S, PACK], BF16, align_bytes=64)
         z_words = keep.tile([P, S], U32, align_bytes=64)
         z_scales = keep.tile([P, S], U8, align_bytes=64)
-        whole = slice(0, S)
-        low, high = slice(0, HALF), slice(HALF, S)
 
         def logarithms(t, cols):
             nc.scalar.activation(logs[:, t, :, cols], sums[:, t, :, cols], ACT.Ln)
 
         def weigh(t, cols):
             nc.scalar.activation(scaled[:, t, cols], logs[:, t, 1, cols], ACT.Copy, scale=gain[:, t : t + 1])
-            nc.vector.scalar_tensor_tensor(
-                z32[:, t, cols], logs[:, t, 0, cols], gain[:, t : t + 1], scaled[:, t, cols], ALU.mult, ALU.subtract
-            )
 
         logarithms(0, whole)
         logarithms(1, whole)
@@ -165,9 +174,13 @@ def tile_picked_candoddshopmx_none_p_kernel(
         logarithms(2, whole)
         logarithms(3, low)
         weigh(2, whole)
-        logarithms(3, high)
         weigh(3, low)
+        logarithms(3, high)
         weigh(3, high)
+        for t, cols in ((0, whole), (1, whole), (2, low), (3, low), (2, high), (3, high)):
+            nc.vector.scalar_tensor_tensor(
+                z32[:, t, cols], logs[:, t, 0, cols], gain[:, t : t + 1], scaled[:, t, cols], ALU.mult, ALU.subtract
+            )
 
         def walk_out(cols):
             return z_bf[:, cols, :].rearrange("p (c i) t -> p c t i", i=4)
@@ -190,8 +203,8 @@ def tile_picked_candoddshopmx_none_p_kernel(
         nc.scalar.copy(walk_out(low), walk_in(low))
         nc.vector.tensor_copy(walk_out(high), walk_in(high))
         s_ps = [psum.tile([P, S], F32, name=f"s_ps{t}") for t in range(PACK)]
-        first_low = y_ps[0][:, low]
-        for cols, acc in ((high, s_ps[0][:, high]), (low, first_low)):
+        first_high = y_ps[0][:, high]
+        for cols, acc in ((low, s_ps[0][:, low]), (high, first_high)):
             nc.vector.quantize_mx(
                 out=z_words[:, cols].bitcast(FP8X4),
                 scales=z_scales[:, cols],
@@ -202,9 +215,6 @@ def tile_picked_candoddshopmx_none_p_kernel(
             scores(s_ps[t][:], t, whole)
 
         out_rows = out.rearrange("(p t) j -> p t j", t=PACK)
-
-        def entries(cols):
-            return slice(cols.start // 16, cols.stop // 16)
 
         def centre(t, cols):
             nc.vector.tensor_tensor(
@@ -223,19 +233,55 @@ def tile_picked_candoddshopmx_none_p_kernel(
             nc.vector.tensor_tensor(scaled[:, t, cols], win_a[t][:, cols], ex2[t][:, cols], ALU.max)
             nc.sync.dma_start(out_rows[:, t, cols], scaled[:, t, cols])
 
-        nc.scalar.activation(win_b[0][:, high], s_ps[0][:, high], ACT.Copy, scale=-0.0625)
-        nc.scalar.activation(twin[0][:, high], s_ps[0][:, high], ACT.Copy, scale=0.0625)
-        nc.vector.tensor_scalar(win_b[0][:, low], first_low, -0.0625, None, ALU.mult)
-        nc.scalar.activation(twin[0][:, low], first_low, ACT.Copy, scale=0.0625)
-        centre(0, high)
+        st_twin = [keep.tile([P, S], F32, name=f"st_twin{t}") for t in range(2)]
+        st_turned = [keep.tile([P, S], F32, name=f"st_turned{t}") for t in range(2)]
+        excess_turned = [keep.tile([P, S], F32, name=f"excess_turned{t}") for t in range(2)]
+        blocks = [slice(b * P, (b + 1) * P) for b in range(PACK)]
+
+        def turn(acc, src):
+            for cols in blocks:
+                nc.tensor.transpose(acc[:, cols], src[:, cols], identity[:])
+
+        def fetch_excess(t):
+            nc.scalar.copy(st_twin[t][:], win_a[t][:, :S])
+            nc.vector.tensor_tensor(ex2[t][:], win_a[t][:].indirect(n5_sb[:]), st_twin[t][:], ALU.subtract)
+
+        def turn_base(t):
+            turn(y_ps[1], st_twin[t])
+            nc.scalar.copy(st_turned[t][:], y_ps[1][:])
+
+        def turn_excess(t):
+            turn(y_ps[2 + t], ex2[t])
+            nc.scalar.activation(excess_turned[t][:], y_ps[2 + t][:], ACT.Relu)
+
+        def add_back(t):
+            acc = s_ps[t]
+            for cols in blocks:
+                nc.tensor.matmul(acc[:, cols], st_turned[t][:, cols], identity[:], start=True, stop=False, is_transpose=True)
+                nc.tensor.matmul(acc[:, cols], excess_turned[t][:, cols], identity[:], start=False, stop=True, is_transpose=True)
+            nc.scalar.copy(scaled[:, t, :], acc[:])
+            nc.scalar.dma_start(out_rows[:, t, :], scaled[:, t, :])
+
+        nc.scalar.activation(win_b[0][:, low], s_ps[0][:, low], ACT.Copy, scale=-0.0625)
+        nc.scalar.activation(twin[0][:, low], s_ps[0][:, low], ACT.Copy, scale=0.0625)
+        nc.vector.tensor_scalar(win_b[0][:, high], first_high, -0.0625, None, ALU.mult)
+        nc.scalar.activation(twin[0][:, high], first_high, ACT.Copy, scale=0.0625)
         centre(0, low)
-        centre_whole(1)
-        fetch(0, whole)
+        centre(0, high)
+        nc.scalar.activation(win_b[1][:, :S], s_ps[1][:], ACT.Copy, scale=-0.0625)
+        for cols in (low, high):
+            nc.scalar.activation(twin[1][:, cols], s_ps[1][:, cols], ACT.Copy, scale=0.0625)
+            centre(1, cols)
+        fetch_excess(0)
         centre_whole(2)
-        finish(0, whole)
-        fetch(1, whole)
+        fetch_excess(1)
+        turn_base(0)
+        turn_excess(0)
         centre_whole(3)
-        finish(1, whole)
+        turn_base(1)
+        add_back(0)
+        turn_excess(1)
+        add_back(1)
         fetch(2, whole)
         fetch(3, low)
         finish(2, whole)

@@ -20,7 +20,7 @@ P = 128
 PACK = 4
 HALF = S // 2
 WINDOW = 2 * S
-SCALAR_TILES = (2, 3)
+SCALAR_TILES = (1, 2, 3)
 
 
 def tile_picked_candoddshopmx_none_p_kernel(
@@ -78,15 +78,18 @@ def tile_picked_candoddshopmx_none_p_kernel(
         def entries(cols):
             return slice(cols.start // 16, cols.stop // 16)
 
+        def deal(dst, src, tiles, run):
+            nc.vector.tensor_copy(
+                dst[:].rearrange("p (t c i) -> p c t i", t=tiles.stop - tiles.start, i=run),
+                src[:].rearrange("p (c i t) -> p c t i", t=PACK, i=run)[:, :, tiles, :],
+            )
+
         xq_scales = keep.tile([P, S], U8, align_bytes=64)
         nc.vector.tensor_copy(xq_scales[:], table_scales[:].indirect(offs_sb[:]))
         cand_scales_raw = keep.tile([P, C], U8, align_bytes=64)
         nc.vector.tensor_copy(cand_scales_raw[:], table_scales[:].indirect(cand_sb[:]))
         cand_scales = keep.tile([P, C], U8, align_bytes=64)
-        nc.vector.tensor_copy(
-            cand_scales[:].rearrange("p (t c i) -> p c t i", t=PACK, i=16),
-            cand_scales_raw[:].rearrange("p (c i t) -> p c t i", t=PACK, i=16),
-        )
+        deal(cand_scales, cand_scales_raw, slice(0, PACK), 16)
 
         w_bf = keep.tile([P, PACK, P, PACK], BF16, align_bytes=64)
         w_walk = w_bf[:].rearrange("p t m j -> p m t j")
@@ -100,37 +103,46 @@ def tile_picked_candoddshopmx_none_p_kernel(
         nc.vector.quantize_mx(
             out=w_words[:].bitcast(FP8X4), scales=w_scales[:], in_=w_bf[:].rearrange("p t m j -> p (t m j)")
         )
+        s_ps = [psum.tile([P, S], F32, name=f"s_ps{t}") for t in range(PACK)]
         xq_words = keep.tile([P, S], U32, align_bytes=64)
-        nc.vector.tensor_copy(xq_words[:], table_words[:].indirect(offs_sb[:]))
-        for t in range(PACK):
-            cols = slice(t * P, (t + 1) * P)
+
+        def project(acc, t, cols):
+            rows = slice(t * P, (t + 1) * P)
             nc.tensor.matmul_mx(
-                out=y_ps[t][:],
-                lhsT=w_words[:, cols].bitcast(FP8X4),
-                lhsT_scale=w_scales[:, cols],
-                rhs=xq_words[:].bitcast(FP8X4),
-                rhs_scale=xq_scales[:],
+                out=acc,
+                lhsT=w_words[:, rows].bitcast(FP8X4),
+                lhsT_scale=w_scales[:, rows],
+                rhs=xq_words[:, cols].bitcast(FP8X4),
+                rhs_scale=xq_scales[:, cols],
                 start=True,
                 stop=True,
             )
 
+        for cols, banks in ((low, y_ps), (high, s_ps)):
+            nc.vector.tensor_copy(xq_words[:, cols], table_words[:].indirect(offs_sb[:, entries(cols)]))
+            for t in (0, 1):
+                project(banks[t][:, cols], t, cols)
+        for t in (2, 3):
+            project(y_ps[t][:], t, whole)
+
         cand_words_raw = keep.tile([P, C], U32, align_bytes=64)
         nc.vector.tensor_copy(cand_words_raw[:], table_words[:].indirect(cand_sb[:]))
-        cand_words = keep.tile([P, C], U32, align_bytes=64)
-        nc.vector.tensor_copy(
-            cand_words[:].rearrange("p (t c i) -> p c t i", t=PACK, i=4),
-            cand_words_raw[:].rearrange("p (c i t) -> p c t i", t=PACK, i=4),
-        )
+        first_words = keep.tile([P, P], U32, align_bytes=64)
+        deal(first_words, cand_words_raw, slice(0, 1), 4)
 
         twin = [keep.tile([P, S], F32, name=f"twin{t}") for t in range(PACK)]
         ex2 = [keep.tile([P, S], F32, name=f"ex2_{t}") for t in range(PACK)]
         sums = keep.tile([P, PACK, 2, S], F32)
+        for cols, banks in ((low, y_ps), (high, s_ps)):
+            nc.scalar.activation(win_a[0][:, cols], banks[0][:, cols], ACT.Exp, scale=0.5)
+            nc.scalar.activation(win_b[1][:, cols], banks[1][:, cols], ACT.Copy, scale=0.5)
+            nc.scalar.activation(win_a[1][:, cols], banks[1][:, cols], ACT.Exp, scale=0.5)
         for t in range(PACK):
-            if t in SCALAR_TILES:
+            if t >= 2:
                 nc.scalar.activation(win_b[t % 2][:, :S], y_ps[t][:], ACT.Copy, scale=0.5)
-            nc.scalar.activation(win_a[t][:, :S], y_ps[t][:], ACT.Exp, scale=0.5)
+                nc.scalar.activation(win_a[t][:, :S], y_ps[t][:], ACT.Exp, scale=0.5)
             nc.sync.dma_start(twin[t][:], win_a[t][:, :S])
-            if t in SCALAR_TILES:
+            if t >= 1:
                 nc.scalar.activation(ex2[t][:], win_b[t % 2][:].indirect(n2_sb[:]), ACT.Exp)
 
         def denominator(t, cols):
@@ -143,12 +155,10 @@ def tile_picked_candoddshopmx_none_p_kernel(
                 sums[:, t, 0, cols], win_a[t][:].indirect(n1_sb[:, entries(cols)]), twin[t][:, cols], ALU.add
             )
 
-        vector_tiles = [t for t in range(PACK) if t not in SCALAR_TILES]
-        for t in vector_tiles:
-            nc.vector.tensor_copy(ex2[t][:], win_a[t][:].indirect(n2_sb[:]))
-        for t in vector_tiles:
+        nc.vector.tensor_copy(ex2[0][:], win_a[0][:].indirect(n2_sb[:]))
+        for t in (0, 1):
             denominator(t, whole)
-        for t in vector_tiles:
+        for t in (0, 1):
             numerator(t, whole)
         for t, cols in ((2, whole), (3, low), (3, high)):
             denominator(t, cols)
@@ -157,7 +167,8 @@ def tile_picked_candoddshopmx_none_p_kernel(
         logs = keep.tile([P, PACK, 2, S], F32)
         scaled = keep.tile([P, PACK, S], F32)
         z32 = keep.tile([P, PACK, S], F32)
-        z_bf = keep.tile([P, S, PACK], BF16, align_bytes=64)
+        z_low = keep.tile([P, HALF, PACK], BF16, align_bytes=64)
+        z_high = keep.tile([P, HALF, PACK], BF16, align_bytes=64, tag="z_high")
         z_words = keep.tile([P, S], U32, align_bytes=64)
         z_scales = keep.tile([P, S], U8, align_bytes=64)
 
@@ -169,50 +180,53 @@ def tile_picked_candoddshopmx_none_p_kernel(
 
         logarithms(0, whole)
         logarithms(1, whole)
-        weigh(0, whole)
-        weigh(1, whole)
         logarithms(2, whole)
-        logarithms(3, low)
         weigh(2, whole)
+        logarithms(3, low)
         weigh(3, low)
         logarithms(3, high)
         weigh(3, high)
-        for t, cols in ((0, whole), (1, whole), (2, low), (3, low), (2, high), (3, high)):
+        for t in (0, 1):
+            nc.vector.tensor_tensor(scaled[:, t, :], logs[:, t, 0, :], logs[:, t, 1, :], ALU.subtract)
+        for t in (0, 1):
+            nc.vector.tensor_scalar(z32[:, t, :], scaled[:, t, :], gain[:, t : t + 1], None, ALU.mult)
+        for t, cols in ((2, low), (3, low), (2, high), (3, high)):
             nc.vector.scalar_tensor_tensor(
                 z32[:, t, cols], logs[:, t, 0, cols], gain[:, t : t + 1], scaled[:, t, cols], ALU.mult, ALU.subtract
             )
 
-        def walk_out(cols):
-            return z_bf[:, cols, :].rearrange("p (c i) t -> p c t i", i=4)
+        def walk_out(z_bf):
+            return z_bf[:].rearrange("p (c i) t -> p c t i", i=4)
 
         def walk_in(cols):
             return z32[:, :, cols].rearrange("p t (c i) -> p c t i", i=4)
 
-        def scores(acc, t, cols):
-            rows = slice(t * P, (t + 1) * P)
+        def scores(acc, words, scales, cols):
             nc.tensor.matmul_mx(
                 out=acc,
-                lhsT=cand_words[:, rows].bitcast(FP8X4),
-                lhsT_scale=cand_scales[:, rows],
+                lhsT=words.bitcast(FP8X4),
+                lhsT_scale=scales,
                 rhs=z_words[:, cols].bitcast(FP8X4),
                 rhs_scale=z_scales[:, cols],
                 start=True,
                 stop=True,
             )
 
-        nc.scalar.copy(walk_out(low), walk_in(low))
-        nc.vector.tensor_copy(walk_out(high), walk_in(high))
-        s_ps = [psum.tile([P, S], F32, name=f"s_ps{t}") for t in range(PACK)]
+        nc.scalar.copy(walk_out(z_low), walk_in(low))
+        nc.vector.tensor_copy(walk_out(z_high), walk_in(high))
         first_high = y_ps[0][:, high]
-        for cols, acc in ((low, s_ps[0][:, low]), (high, first_high)):
+        for cols, z_bf, acc in ((low, z_low, s_ps[0][:, low]), (high, z_high, first_high)):
             nc.vector.quantize_mx(
                 out=z_words[:, cols].bitcast(FP8X4),
                 scales=z_scales[:, cols],
-                in_=z_bf[:, cols, :].rearrange("p j t -> p (j t)"),
+                in_=z_bf[:].rearrange("p j t -> p (j t)"),
             )
-            scores(acc, 0, cols)
+            scores(acc, first_words[:], cand_scales[:, :P], cols)
+        rest_words = keep.tile([P, C - P], U32, align_bytes=64, tag="z_high")
+        deal(rest_words, cand_words_raw, slice(1, PACK), 4)
         for t in range(1, PACK):
-            scores(s_ps[t][:], t, whole)
+            rows = slice((t - 1) * P, t * P)
+            scores(s_ps[t][:], rest_words[:, rows], cand_scales[:, t * P : (t + 1) * P], whole)
 
         out_rows = out.rearrange("(p t) j -> p t j", t=PACK)
 
@@ -229,9 +243,9 @@ def tile_picked_candoddshopmx_none_p_kernel(
         def fetch(t, cols):
             nc.vector.tensor_copy(ex2[t][:, cols], win_a[t][:].indirect(n5_sb[:, entries(cols)]))
 
-        def finish(t, cols):
+        def finish(t, cols, queue):
             nc.vector.tensor_tensor(scaled[:, t, cols], win_a[t][:, cols], ex2[t][:, cols], ALU.max)
-            nc.sync.dma_start(out_rows[:, t, cols], scaled[:, t, cols])
+            queue.dma_start(out_rows[:, t, cols], scaled[:, t, cols])
 
         st_twin = [keep.tile([P, S], F32, name=f"st_twin{t}") for t in range(2)]
         st_turned = [keep.tile([P, S], F32, name=f"st_turned{t}") for t in range(2)]
@@ -273,18 +287,18 @@ def tile_picked_candoddshopmx_none_p_kernel(
             nc.scalar.activation(twin[1][:, cols], s_ps[1][:, cols], ACT.Copy, scale=0.0625)
             centre(1, cols)
         fetch_excess(0)
-        centre_whole(2)
         fetch_excess(1)
-        turn_base(0)
-        turn_excess(0)
+        centre_whole(2)
         centre_whole(3)
-        turn_base(1)
-        add_back(0)
-        turn_excess(1)
-        add_back(1)
         fetch(2, whole)
         fetch(3, low)
-        finish(2, whole)
+        finish(2, whole, nc.sync)
         fetch(3, high)
-        finish(3, low)
-        finish(3, high)
+        turn_base(0)
+        turn_excess(0)
+        turn_base(1)
+        turn_excess(1)
+        add_back(0)
+        add_back(1)
+        finish(3, low, nc.sync)
+        finish(3, high, nc.sync)

from contextlib import ExitStack

import concourse.mybir as mybir
from concourse.masks import make_identity

K, T, S, H, C = 512, 2048, 512, 512, 512
FLOPS = 2 * K * H * S + 2 * H * C * S

F32 = mybir.dt.float32
BF16 = mybir.dt.bfloat16
I32 = mybir.dt.int32
U32 = mybir.dt.uint32
U16 = mybir.dt.uint16
U8 = mybir.dt.uint8
FP8X4 = mybir.dt.float8_e4m3fn_x4
ACT = mybir.ActivationFunctionType
ALU = mybir.AluOpType

P = 128
PACK = 4
HALF = S // 2
WINDOW = 2 * S
SCALAR_TILES = (1, 2, 3)


def tile_picked_candoddshopmx_none_p_kernel(
    tc, x_words, x_scales, w1, gs, offs, n1, n2, n3, cand, n4, n5, out
):
    nc = tc.nc
    with ExitStack() as ctx:
        lists = ctx.enter_context(tc.tile_pool(name="lists", bufs=1))
        keep = ctx.enter_context(tc.tile_pool(name="keep", bufs=1))
        psum = ctx.enter_context(tc.psum_pool(name="psum", bufs=1))

        def load_list(src, name):
            tile = lists.tile([P, S // 16], U16, name=name)
            nc.sync.dma_start(tile[:], src)
            return tile

        table_scales = keep.tile([P, T], U8, align_bytes=64)
        nc.gpsimd.memset(table_scales[:].bitcast(I32), 0)
        w_rows = w1.rearrange("(p j) c -> p j c", j=PACK)
        w_raw = [keep.tile([P, PACK, H // 2], F32, name=f"w_raw{u}") for u in range(2)]
        nc.sync.dma_start(w_raw[0][:], w_rows[:, :, : H // 2])
        for q in range(4):
            nc.sync.dma_start(
                table_scales[32 * q : 32 * q + 4, :].bitcast(I32),
                x_scales[0, 4 * q : 4 * q + 4, :].bitcast(I32),
            )
        offs_sb = load_list(offs, "offs_sb")
        cand_sb = load_list(cand, "cand_sb")
        nc.sync.dma_start(w_raw[1][:], w_rows[:, :, H // 2 :])
        table_words = keep.tile([P, T], U32, align_bytes=64)
        nc.sync.dma_start(
            table_words[:].bitcast(I32), x_words[0].rearrange("p n r -> p (n r)").bitcast(I32)
        )
        n2_sb = load_list(n2, "n2_sb")
        n3_sb = load_list(n3, "n3_sb")
        n1_sb = load_list(n1, "n1_sb")
        gain = keep.tile([P, PACK], F32)
        nc.sync.dma_start(gain[:], gs.rearrange("(p t) o -> p (t o)", t=PACK))
        n4_sb = load_list(n4, "n4_sb")
        n5_sb = load_list(n5, "n5_sb")

        win_a = [keep.tile([P, WINDOW], F32, name=f"win_a{t}") for t in range(PACK)]
        win_b = [keep.tile([P, WINDOW], F32, name=f"win_b{t}") for t in range(2)]
        for win in win_a[:3]:
            nc.vector.memset(win[:, S:], 0.0)
        for win in win_a[3:] + win_b:
            nc.gpsimd.memset(win[:, S:], 0.0)

        identity = keep.tile([P, P], F32)
        make_identity(nc, identity[:])

        whole = slice(0, S)
        low, high = slice(0, HALF), slice(HALF, S)

        def entries(cols):
            return slice(cols.start // 16, cols.stop // 16)

        def deal(dst, src, tiles, run):
            nc.vector.tensor_copy(
                dst[:].rearrange("p (t c i) -> p c t i", t=tiles.stop - tiles.start, i=run),
                src[:].rearrange("p (c i t) -> p c t i", t=PACK, i=run)[:, :, tiles, :],
            )

        xq_scales = keep.tile([P, S], U8, align_bytes=64)
        nc.vector.tensor_copy(xq_scales[:], table_scales[:].indirect(offs_sb[:]))
        cand_scales_raw = keep.tile([P, C], U8, align_bytes=64)
        nc.vector.tensor_copy(cand_scales_raw[:], table_scales[:].indirect(cand_sb[:]))
        cand_scales = keep.tile([P, C], U8, align_bytes=64)
        deal(cand_scales, cand_scales_raw, slice(0, PACK), 16)

        w_bf = keep.tile([P, PACK, P, PACK], BF16, align_bytes=64)
        w_walk = w_bf[:].rearrange("p t m j -> p m t j")
        for u in range(2):
            nc.scalar.copy(
                w_walk[:, u * (P // 2) : (u + 1) * (P // 2)], w_raw[u][:].rearrange("p j (m t) -> p m t j", t=PACK)
            )
        w_words = keep.tile([P, H], U32, align_bytes=64)
        w_scales = keep.tile([P, H], U8, align_bytes=64)
        y_ps = [psum.tile([P, S], F32, name=f"y_ps{t}") for t in range(PACK)]
        nc.vector.quantize_mx(
            out=w_words[:].bitcast(FP8X4), scales=w_scales[:], in_=w_bf[:].rearrange("p t m j -> p (t m j)")
        )
        s_ps = [psum.tile([P, S], F32, name=f"s_ps{t}") for t in range(PACK)]
        xq_words = keep.tile([P, S], U32, align_bytes=64)

        def project(acc, t, cols):
            rows = slice(t * P, (t + 1) * P)
            nc.tensor.matmul_mx(
                out=acc,
                lhsT=w_words[:, rows].bitcast(FP8X4),
                lhsT_scale=w_scales[:, rows],
                rhs=xq_words[:, cols].bitcast(FP8X4),
                rhs_scale=xq_scales[:, cols],
                start=True,
                stop=True,
            )

        for cols, banks in ((low, y_ps), (high, s_ps)):
            nc.vector.tensor_copy(xq_words[:, cols], table_words[:].indirect(offs_sb[:, entries(cols)]))
            for t in (0, 1):
                project(banks[t][:, cols], t, cols)
        for t in (2, 3):
            project(y_ps[t][:], t, whole)

        cand_words_raw = keep.tile([P, C], U32, align_bytes=64)
        nc.vector.tensor_copy(cand_words_raw[:], table_words[:].indirect(cand_sb[:]))
        first_words = keep.tile([P, P], U32, align_bytes=64)
        deal(first_words, cand_words_raw, slice(0, 1), 4)

        twin = [keep.tile([P, S], F32, name=f"twin{t}") for t in range(PACK)]
        ex2 = [keep.tile([P, S], F32, name=f"ex2_{t}") for t in range(PACK)]
        sums = keep.tile([P, PACK, 2, S], F32)
        for cols, banks in ((low, y_ps), (high, s_ps)):
            nc.scalar.activation(win_a[0][:, cols], banks[0][:, cols], ACT.Exp, scale=0.5)
            nc.scalar.activation(win_b[1][:, cols], banks[1][:, cols], ACT.Copy, scale=0.5)
            nc.scalar.activation(win_a[1][:, cols], banks[1][:, cols], ACT.Exp, scale=0.5)
        for t in range(PACK):
            if t >= 2:
                nc.scalar.activation(win_b[t % 2][:, :S], y_ps[t][:], ACT.Copy, scale=0.5)
                nc.scalar.activation(win_a[t][:, :S], y_ps[t][:], ACT.Exp, scale=0.5)
            nc.sync.dma_start(twin[t][:], win_a[t][:, :S])
            if t >= 1:
                nc.scalar.activation(ex2[t][:], win_b[t % 2][:].indirect(n2_sb[:]), ACT.Exp)

        def denominator(t, cols):
            nc.vector.tensor_tensor(
                sums[:, t, 1, cols], win_a[t][:].indirect(n3_sb[:, entries(cols)]), ex2[t][:, cols], ALU.add
            )

        def numerator(t, cols):
            nc.vector.tensor_tensor(
                sums[:, t, 0, cols], win_a[t][:].indirect(n1_sb[:, entries(cols)]), twin[t][:, cols], ALU.add
            )

        nc.vector.tensor_copy(ex2[0][:], win_a[0][:].indirect(n2_sb[:]))
        for t in (0, 1):
            denominator(t, whole)
        for t in (0, 1):
            numerator(t, whole)
        for t, cols in ((2, whole), (3, low), (3, high)):
            denominator(t, cols)
            numerator(t, cols)

        logs = keep.tile([P, PACK, 2, S], F32)
        scaled = keep.tile([P, PACK, S], F32)
        z32 = keep.tile([P, PACK, S], F32)
        z_low = keep.tile([P, HALF, PACK], BF16, align_bytes=64)
        z_high = keep.tile([P, HALF, PACK], BF16, align_bytes=64, tag="z_high")
        z_words = keep.tile([P, S], U32, align_bytes=64)
        z_scales = keep.tile([P, S], U8, align_bytes=64)

        def logarithms(t, cols):
            nc.scalar.activation(logs[:, t, :, cols], sums[:, t, :, cols], ACT.Ln)

        def weigh(t, cols):
            nc.scalar.activation(scaled[:, t, cols], logs[:, t, 1, cols], ACT.Copy, scale=gain[:, t : t + 1])

        logarithms(0, whole)
        logarithms(1, whole)
        logarithms(2, whole)
        weigh(2, whole)
        logarithms(3, low)
        weigh(3, low)
        logarithms(3, high)
        weigh(3, high)
        for t in (0, 1):
            nc.vector.tensor_tensor(scaled[:, t, :], logs[:, t, 0, :], logs[:, t, 1, :], ALU.subtract)
        for t in (0, 1):
            nc.vector.tensor_scalar(z32[:, t, :], scaled[:, t, :], gain[:, t : t + 1], None, ALU.mult)
        for t, cols in ((2, low), (3, low), (2, high), (3, high)):
            nc.vector.scalar_tensor_tensor(
                z32[:, t, cols], logs[:, t, 0, cols], gain[:, t : t + 1], scaled[:, t, cols], ALU.mult, ALU.subtract
            )

        def walk_out(z_bf):
            return z_bf[:].rearrange("p (c i) t -> p c t i", i=4)

        def walk_in(cols):
            return z32[:, :, cols].rearrange("p t (c i) -> p c t i", i=4)

        def scores(acc, words, scales, cols):
            nc.tensor.matmul_mx(
                out=acc,
                lhsT=words.bitcast(FP8X4),
                lhsT_scale=scales,
                rhs=z_words[:, cols].bitcast(FP8X4),
                rhs_scale=z_scales[:, cols],
                start=True,
                stop=True,
            )

        nc.scalar.copy(walk_out(z_low), walk_in(low))
        nc.vector.tensor_copy(walk_out(z_high), walk_in(high))
        first_high = y_ps[0][:, high]
        for cols, z_bf, acc in ((low, z_low, s_ps[0][:, low]), (high, z_high, first_high)):
            nc.vector.quantize_mx(
                out=z_words[:, cols].bitcast(FP8X4),
                scales=z_scales[:, cols],
                in_=z_bf[:].rearrange("p j t -> p (j t)"),
            )
            scores(acc, first_words[:], cand_scales[:, :P], cols)
        rest_words = keep.tile([P, C - P], U32, align_bytes=64, tag="z_high")
        deal(rest_words, cand_words_raw, slice(1, PACK), 4)
        for t in range(1, PACK):
            rows = slice((t - 1) * P, t * P)
            scores(s_ps[t][:], rest_words[:, rows], cand_scales[:, t * P : (t + 1) * P], whole)

        out_rows = out.rearrange("(p t) j -> p t j", t=PACK)

        def centre(t, cols):
            nc.vector.tensor_tensor(
                win_a[t][:, cols], win_b[t % 2][:].indirect(n4_sb[:, entries(cols)]), twin[t][:, cols], ALU.add
            )

        def centre_whole(t):
            nc.scalar.activation(win_b[t % 2][:, :S], s_ps[t][:], ACT.Copy, scale=-0.0625)
            nc.scalar.activation(twin[t][:], s_ps[t][:], ACT.Copy, scale=0.0625)
            centre(t, whole)

        def fetch(t, cols):
            nc.vector.tensor_copy(ex2[t][:, cols], win_a[t][:].indirect(n5_sb[:, entries(cols)]))

        def finish(t, cols, queue):
            nc.vector.tensor_tensor(scaled[:, t, cols], win_a[t][:, cols], ex2[t][:, cols], ALU.max)
            queue.dma_start(out_rows[:, t, cols], scaled[:, t, cols])

        st_twin = [keep.tile([P, S], F32, name=f"st_twin{t}") for t in range(2)]
        st_turned = [keep.tile([P, S], F32, name=f"st_turned{t}") for t in range(2)]
        excess_turned = [keep.tile([P, S], F32, name=f"excess_turned{t}") for t in range(2)]
        blocks = [slice(b * P, (b + 1) * P) for b in range(PACK)]

        def turn(acc, src):
            for cols in blocks:
                nc.tensor.transpose(acc[:, cols], src[:, cols], identity[:])

        def fetch_excess(t):
            nc.scalar.copy(st_twin[t][:], win_a[t][:, :S])
            nc.vector.tensor_tensor(ex2[t][:], win_a[t][:].indirect(n5_sb[:]), st_twin[t][:], ALU.subtract)

        def turn_base(t):
            turn(y_ps[1], st_twin[t])
            nc.scalar.copy(st_turned[t][:], y_ps[1][:])

        def turn_excess(t):
            turn(y_ps[2 + t], ex2[t])
            nc.scalar.activation(excess_turned[t][:], y_ps[2 + t][:], ACT.Relu)

        def add_back(t):
            acc = s_ps[t]
            for cols in blocks:
                nc.tensor.matmul(acc[:, cols], st_turned[t][:, cols], identity[:], start=True, stop=False, is_transpose=True)
                nc.tensor.matmul(acc[:, cols], excess_turned[t][:, cols], identity[:], start=False, stop=True, is_transpose=True)
            nc.scalar.copy(scaled[:, t, :], acc[:])
            nc.scalar.dma_start(out_rows[:, t, :], scaled[:, t, :])

        nc.scalar.activation(win_b[0][:, low], s_ps[0][:, low], ACT.Copy, scale=-0.0625)
        nc.scalar.activation(twin[0][:, low], s_ps[0][:, low], ACT.Copy, scale=0.0625)
        nc.vector.tensor_scalar(win_b[0][:, high], first_high, -0.0625, None, ALU.mult)
        nc.scalar.activation(twin[0][:, high], first_high, ACT.Copy, scale=0.0625)
        centre(0, low)
        centre(0, high)
        nc.scalar.activation(win_b[1][:, :S], s_ps[1][:], ACT.Copy, scale=-0.0625)
        for cols in (low, high):
            nc.scalar.activation(twin[1][:, cols], s_ps[1][:, cols], ACT.Copy, scale=0.0625)
            centre(1, cols)
        fetch_excess(0)
        fetch_excess(1)
        centre_whole(2)
        centre_whole(3)
        fetch(2, whole)
        fetch(3, low)
        finish(2, whole, nc.sync)
        fetch(3, high)
        turn_base(0)
        turn_excess(0)
        turn_base(1)
        turn_excess(1)
        add_back(0)
        add_back(1)
        finish(3, low, nc.sync)
        finish(3, high, nc.sync)
